import numpy as np
import ml_dtypes


def mxq(x, axis, fmt="e4m3"):
    dtype, down = {"e4m3": (ml_dtypes.float8_e4m3fn, 7), "e5m2": (ml_dtypes.float8_e5m2, 14)}[fmt]
    v = np.moveaxis(np.asarray(x, np.float32).astype(ml_dtypes.bfloat16).astype(np.float64), axis, -1)
    blocks = v.reshape(v.shape[:-1] + (-1, 32))
    amax = np.abs(blocks).max(-1, keepdims=True)
    byte = np.maximum(np.where(amax > 0, np.frexp(amax)[1] - 1 + 127, 0) - down, 1)
    scale = np.exp2(byte - 127.0)
    codes = (blocks / scale).astype(np.float32).astype(dtype).astype(np.float64)
    return np.moveaxis((codes * scale).reshape(v.shape), -1, axis)


WIDE = False


def mx_kscale(k):
    if not WIDE:
        return np.ones(k)
    levels = np.array([10, -10, 5, -5, 0])
    if k % 512:
        return np.exp2(np.random.permutation(np.resize(levels, k // 32))).repeat(32)
    a = np.empty((k // 512, 16))
    for p in range(k // 512):
        a[p, :8] = np.random.permutation(np.resize(levels, 8))
        for g in range(8):
            far = levels[np.abs(levels - a[p, g]) >= 10]
            a[p, g + 8] = far[np.random.randint(len(far))]
    return np.exp2(a.ravel()).repeat(32)


def f64(x):
    return np.asarray(x).astype(np.float64)


def striped(idx):
    return np.tile(idx.reshape(-1, 16).T, (8, 1)).astype(np.uint16)


def unstriped(offs):
    return offs[:16].T.reshape(-1).astype(np.int64)


def pack_weight(w):
    k, n = w.shape
    w = f64(np.asarray(w, np.float32).astype(ml_dtypes.bfloat16)).reshape(k // 32, 32, n)
    amax = np.abs(w).max(1)
    byte = np.clip(np.where(amax > 0, np.frexp(amax)[1] - 1 + 127 - 7, 1), 1, 254)
    scaled = (w * np.exp2(127.0 - byte)[:, None, :]).reshape(k, n).astype(np.float32)
    words = np.ascontiguousarray(scaled.reshape(k // 512, 128, 4, n).transpose(0, 1, 3, 2)).astype(ml_dtypes.float8_e4m3fn).view(np.uint8)
    return words, np.ascontiguousarray(byte.astype(np.uint8).reshape(k // 512, 16, n))


def unpack_weight(words, scales):
    g, p, n, _ = words.shape
    vals = np.ascontiguousarray(words).view(ml_dtypes.float8_e4m3fn).astype(np.float64) * np.repeat(np.exp2(scales.astype(np.float64) - 127.0), 8, axis=1)[..., None]
    return vals.transpose(0, 1, 3, 2).reshape(g * 512, n)


def sigmoid(v):
    return 1.0 / (1.0 + np.exp(-np.maximum(v, -700.0)))


K, T, S, N, D, V, U = 512, 2048, 512, 128, 4, 256, 1024
P = 2 ** 7


def setup_inputs():
    n = np.random.standard_normal
    s = mx_kscale(K)[:, None]
    packed_xT = pack_weight(n((K, T)) * s)
    return {
        "x_words": packed_xT[0],
        "x_scales": packed_xT[1],
        "w1": (n((K, N)) / np.sqrt(K) / s).astype(np.float32),
        "w2": (n((K, N)) / np.sqrt(K) / s).astype(np.float32),
        "one": (np.tile(np.random.uniform(0.8, 1.0, U), (P, 1))).astype(np.float32),
        "offs": striped(np.random.permutation(T)[:S]),
        "opp": striped(np.random.permutation(np.concatenate([np.arange(S), np.random.randint(0, S, U - S)]))),
        "who": striped(np.random.permutation(S)[:V]),
    }


def reference(x_words, x_scales, w1, w2, one, offs, opp, who):
    xq = unpack_weight(x_words, x_scales)[:, unstriped(offs)]
    yd = mxq(f64(w2), 0, "e4m3").T @ xq
    dev = np.log(np.exp(yd) + 1.0) + 0.3
    de = dev[:, unstriped(who)]
    dop = dev[:, unstriped(opp)]
    gw = f64(one)[:1] / (np.sqrt(0.304 * ((dop) ** 2) + 1.0))
    yr = mxq(f64(w1), 0, "e4m3").T @ xq
    me = yr[:, unstriped(who)]
    mo = yr[:, unstriped(opp)]
    ex = sigmoid(gw * (np.repeat(me, D, axis=1) - mo))
    gi = (((gw) ** 2) * ex) * (-1.0 * ex + 1.0)
    iv = gi.reshape(len(gi), -1, D).sum(axis=2)
    nv = ((de) ** 2) / (((de) ** 2) * iv + 1.0)
    ab = np.abs(ex - 0.5)
    return np.sqrt(nv) + 0.5 * (ab.reshape(len(ab), -1, D).max(axis=2))

@@ -1,0 +1,196 @@
+from contextlib import ExitStack
+
+import concourse.mybir as mybir
+
+K, T, S, N, D, V, U = 512, 2048, 512, 128, 4, 256, 1024
+P = 128
+FLOPS = 2 * 2 * K * N * S
+
+F32 = mybir.dt.float32
+BF16 = mybir.dt.bfloat16
+I32 = mybir.dt.int32
+U32 = mybir.dt.uint32
+U16 = mybir.dt.uint16
+U8 = mybir.dt.uint8
+FP8X4 = mybir.dt.float8_e4m3fn_x4
+ALU = mybir.AluOpType
+ACT = mybir.ActivationFunctionType
+AXIS = mybir.AxisListType
+
+HALF = S // 2
+CH = 256
+NCH = U // CH
+VCH = CH // D
+TINY = 2.0 ** -60
+
+
+def tile_picked_yglick_dev_p_kernel(tc, x_words, x_scales, w1, w2, one, offs, opp, who, out):
+    nc = tc.nc
+    with ExitStack() as ctx:
+        keep = ctx.enter_context(tc.tile_pool(name="keep", bufs=1))
+        psum = ctx.enter_context(tc.psum_pool(name="psum", bufs=1))
+
+        offs_t = keep.tile([P, S // 16], U16, name="offs_t")
+        opp_t = keep.tile([P, U // 16], U16, name="opp_t")
+        who_t = keep.tile([P, V // 16], U16, name="who_t")
+        all_scales = keep.tile([P, T], U8, name="all_scales", align_bytes=64)
+        all_words = keep.tile([P, T], U32, name="all_words", align_bytes=64)
+        w2_raw = keep.tile([P, 4, N], F32, name="w2_raw")
+        w1_raw = keep.tile([P, 4, N], F32, name="w1_raw", tag="stage")
+
+        nc.vector.memset(all_scales[:, : T // 2].bitcast(I32), 0)
+        nc.gpsimd.memset(all_scales[:, T // 2 :].bitcast(I32), 0)
+        warm = keep.tile([P, 8], F32, name="warm")
+        warm_out = keep.tile([P, 8], F32, name="warm_out")
+        nc.vector.memset(warm[:], 1.0)
+        nc.scalar.activation(warm_out[:, 0:1], warm[:, 0:1], ACT.Sigmoid)
+
+        nc.sync.dma_start(offs_t[:], offs)
+        nc.sync.dma_start(w1_raw[:], w1.rearrange("(p j) n -> p j n", j=4))
+        for q in range(4):
+            nc.sync.dma_start(all_scales[32 * q : 32 * q + 4, :].bitcast(I32), x_scales[0, 4 * q : 4 * q + 4, :].bitcast(I32))
+        nc.sync.dma_start(all_words[:].bitcast(I32), x_words[0].rearrange("p n t -> p (n t)").bitcast(I32))
+        nc.sync.dma_start(w2_raw[:], w2.rearrange("(p j) n -> p j n", j=4))
+        nc.sync.dma_start(who_t[:], who)
+        nc.sync.dma_start(opp_t[:], opp)
+
+        def quantise(raw, label, copy):
+            grouped = keep.tile([P, N, 4], BF16, name=label + "_bf", align_bytes=64)
+            copy(grouped[:].rearrange("p (c i) j -> p c j i", i=4), raw[:].rearrange("p j (c i) -> p c j i", i=4))
+            codes = keep.tile([P, N], U32, name=label + "_codes", align_bytes=64)
+            scales = keep.tile([P, N], U8, name=label + "_scales", align_bytes=64)
+            nc.vector.quantize_mx(out=codes[:].bitcast(FP8X4), scales=scales[:], in_=grouped[:].rearrange("p n j -> p (n j)"))
+            return codes, scales
+
+        w1_codes, w1_scales = quantise(w1_raw, "w1", nc.vector.tensor_copy)
+        one_t = keep.tile([P, U], F32, name="one_t", tag="stage")
+        nc.sync.dma_start(one_t[:], one)
+
+        x_sc = keep.tile([P, S], U8, name="x_sc", align_bytes=64)
+        nc.vector.tensor_copy(x_sc[:], all_scales[:].indirect(offs_t[:]))
+        x_w = [keep.tile([P, HALF], U32, name=f"x_w{h}", align_bytes=64) for h in range(2)]
+        for h in range(2):
+            nc.vector.tensor_copy(x_w[h][:], all_words[:].indirect(offs_t[:, 16 * h : 16 * (h + 1)]))
+        w2_codes, w2_scales = quantise(w2_raw, "w2", nc.scalar.copy)
+
+        def product(codes, scales, h, label):
+            acc = psum.tile([P, HALF], F32, name=f"{label}{h}")
+            nc.tensor.matmul_mx(out=acc[:], lhsT=codes[:].bitcast(FP8X4), lhsT_scale=scales[:],
+                                rhs=x_w[h][:].bitcast(FP8X4), rhs_scale=x_sc[:, HALF * h : HALF * (h + 1)],
+                                start=True, stop=True)
+            return acc
+
+        yr_ps = [product(w1_codes, w1_scales, h, "yr") for h in range(2)]
+        yd = [product(w2_codes, w2_scales, h, "yd") for h in range(2)]
+
+        sig = keep.tile([P, S], F32, name="sig")
+        lns = keep.tile([P, S], F32, name="lns")
+        soft = keep.tile([P, S], F32, name="soft")
+        xsq = keep.tile([P, S], F32, name="xsq")
+        g0 = keep.tile([P, S], F32, name="g0")
+        yr = keep.tile([P, S], F32, name="yr")
+        cols = [slice(HALF * h, HALF * (h + 1)) for h in range(2)]
+        nc.scalar.copy(yr[:, cols[0]], yr_ps[0][:])
+        nc.vector.tensor_copy(yr[:, cols[1]], yr_ps[1][:])
+        for h in range(2):
+            nc.scalar.activation(sig[:, cols[h]], yd[h][:], ACT.Sigmoid, scale=-1.0)
+        nc.scalar.activation(lns[:], sig[:], ACT.Ln, bias=TINY)
+
+        me = keep.tile([P, V], F32, name="me")
+        nc.vector.tensor_copy(me[:], yr[:].indirect(who_t[:]))
+        me_rep = keep.tile([P, V, D], F32, name="me_rep")
+        nc.vector.tensor_copy(me_rep[:], me[:].unsqueeze(2).to_broadcast([P, V, D]))
+        me_flat = me_rep[:].rearrange("p v d -> p (v d)")
+
+        diff_a = keep.tile([P, 2 * CH], F32, name="diff_a")
+        diff = [diff_a[:, :CH], diff_a[:, CH:], soft[:, :CH], soft[:, CH:]]
+        gw = keep.tile([P, U], F32, name="gw")
+        u = keep.tile([P, U], F32, name="u")
+        th = keep.tile([P, U], F32, name="th")
+        th2 = keep.tile([P, U], F32, name="th2")
+        gw2 = keep.tile([P, U], F32, name="gw2")
+        gi = keep.tile([P, U], F32, name="gi")
+        games = [slice(CH * c, CH * (c + 1)) for c in range(NCH)]
+        rated = [slice(VCH * c, VCH * (c + 1)) for c in range(NCH)]
+        lists = [opp_t[:, 16 * c : 16 * (c + 1)] for c in range(NCH)]
+
+        def gather_diff(c):
+            nc.vector.tensor_tensor(diff[c], yr[:].indirect(lists[c]), me_flat[:, games[c]], ALU.subtract)
+
+        def gather_gw(c):
+            nc.vector.tensor_tensor(gw[:, games[c]], g0[:].indirect(lists[c]), one_t[:, games[c]], ALU.mult)
+
+        def logit(c):
+            nc.vector.tensor_tensor(u[:, games[c]], gw[:, games[c]], diff[c], ALU.mult)
+
+        gather_diff(0)
+        gather_diff(1)
+        for h in range(2):
+            nc.vector.scalar_tensor_tensor(soft[:, cols[h]], lns[:, cols[h]], -1.0, yd[h][:], ALU.mult, ALU.max)
+        for h in range(2):
+            nc.vector.scalar_tensor_tensor(xsq[:, cols[h]], soft[:, cols[h]], 0.6, soft[:, cols[h]], ALU.add, ALU.mult)
+        nc.scalar.activation(g0[:], xsq[:], ACT.Abs_reciprocal_sqrt, scale=0.304, bias=1.0 + 0.304 * 0.09)
+        rd = keep.tile([P, S], F32, name="rd")
+        rd2 = keep.tile([P, S], F32, name="rd2")
+        nc.scalar.activation(rd[:], xsq[:], ACT.Abs_reciprocal_sqrt, bias=0.09)
+        gather_diff(2)
+        gather_gw(0)
+        gather_gw(1)
+        logit(0)
+        logit(1)
+        gather_gw(2)
+        gather_diff(3)
+        logit(2)
+        gather_gw(3)
+
+        amax = keep.tile([P, V], F32, name="amax")
+        niv = keep.tile([P, V], F32, name="niv")
+        info = keep.tile([P, V], F32, name="info")
+
+        def curves(c):
+            nc.scalar.activation(th[:, games[c]], u[:, games[c]], ACT.Tanh, scale=0.5)
+            nc.scalar.activation(gw2[:, games[c]], gw[:, games[c]], ACT.Square)
+            nc.scalar.activation(th2[:, games[c]], th[:, games[c]], ACT.Square)
+
+        def by_rated(t, c):
+            return t[:, games[c]].rearrange("p (v d) -> p v d", d=D)
+
+        def game_info(c):
+            nc.vector.scalar_tensor_tensor(gi[:, games[c]], th2[:, games[c]], 1.0, gw2[:, games[c]], ALU.subtract, ALU.mult)
+
+        def largest(c):
+            nc.vector.tensor_reduce(amax[:, rated[c]], by_rated(th, c), AXIS.X, ALU.max, apply_absolute_value=True)
+
+        def total(c):
+            nc.vector.tensor_reduce(niv[:, rated[c]], by_rated(gi, c), AXIS.X, ALU.add)
+
+        def precision(h):
+            half = slice(V // 2 * h, V // 2 * (h + 1))
+            nc.vector.tensor_tensor(info[:, half], rd2[:].indirect(who_t[:, 8 * h : 8 * (h + 1)]), niv[:, half], ALU.subtract)
+
+        curves(0)
+        game_info(0)
+        logit(3)
+        curves(1)
+        curves(2)
+        nc.scalar.activation(rd2[:], rd[:], ACT.Square, scale=2.0)
+        curves(3)
+        nc.scalar.activation(warm_out[:, 1:2], th2[:, U - 1 : U], ACT.Abs_reciprocal_sqrt, bias=1.0)
+        total(0)
+        game_info(1)
+        largest(0)
+        total(1)
+        game_info(2)
+        largest(1)
+        total(2)
+        precision(0)
+        game_info(3)
+        largest(2)
+        total(3)
+        largest(3)
+        precision(1)
+        root = keep.tile([P, V], F32, name="root")
+        nc.scalar.activation(root[:], info[:], ACT.Abs_reciprocal_sqrt, scale=0.25)
+        res = keep.tile([P, V], F32, name="res")
+        nc.vector.scalar_tensor_tensor(res[:], amax[:], 0.25, root[:], ALU.mult, ALU.add)
+        nc.sync.dma_start(out, res[:])

@@ -35,8 +35,8 @@ def tile_picked_yglick_dev_p_kernel(tc, x_words, x_scales, w1, w2, one, offs, op
         who_t = keep.tile([P, V // 16], U16, name="who_t")
         all_scales = keep.tile([P, T], U8, name="all_scales", align_bytes=64)
         all_words = keep.tile([P, T], U32, name="all_words", align_bytes=64)
+        w1_raw = keep.tile([P, 4, N], F32, name="w1_raw", tag="w1_then_one")
         w2_raw = keep.tile([P, 4, N], F32, name="w2_raw")
-        w1_raw = keep.tile([P, 4, N], F32, name="w1_raw", tag="stage")
 
         nc.vector.memset(all_scales[:, : T // 2].bitcast(I32), 0)
         nc.gpsimd.memset(all_scales[:, T // 2 :].bitcast(I32), 0)
@@ -55,7 +55,7 @@ def tile_picked_yglick_dev_p_kernel(tc, x_words, x_scales, w1, w2, one, offs, op
         nc.sync.dma_start(opp_t[:], opp)
 
         def quantise(raw, label, copy):
-            grouped = keep.tile([P, N, 4], BF16, name=label + "_bf", align_bytes=64)
+            grouped = keep.tile([P, N, 4], BF16, name=label + "_bf", tag=label + "_bf", align_bytes=64)
             copy(grouped[:].rearrange("p (c i) j -> p c j i", i=4), raw[:].rearrange("p j (c i) -> p c j i", i=4))
             codes = keep.tile([P, N], U32, name=label + "_codes", align_bytes=64)
             scales = keep.tile([P, N], U8, name=label + "_scales", align_bytes=64)
@@ -63,134 +63,140 @@ def tile_picked_yglick_dev_p_kernel(tc, x_words, x_scales, w1, w2, one, offs, op
             return codes, scales
 
         w1_codes, w1_scales = quantise(w1_raw, "w1", nc.vector.tensor_copy)
-        one_t = keep.tile([P, U], F32, name="one_t", tag="stage")
+        one_t = keep.tile([P, U], F32, name="one_t", tag="w1_then_one")
         nc.sync.dma_start(one_t[:], one)
 
         x_sc = keep.tile([P, S], U8, name="x_sc", align_bytes=64)
         nc.vector.tensor_copy(x_sc[:], all_scales[:].indirect(offs_t[:]))
-        x_w = [keep.tile([P, HALF], U32, name=f"x_w{h}", align_bytes=64) for h in range(2)]
+        x_w = keep.tile([P, S], U32, name="x_w", align_bytes=64)
         for h in range(2):
-            nc.vector.tensor_copy(x_w[h][:], all_words[:].indirect(offs_t[:, 16 * h : 16 * (h + 1)]))
+            nc.vector.tensor_copy(x_w[:, HALF * h : HALF * (h + 1)], all_words[:].indirect(offs_t[:, 16 * h : 16 * (h + 1)]))
         w2_codes, w2_scales = quantise(w2_raw, "w2", nc.scalar.copy)
 
-        def product(codes, scales, h, label):
-            acc = psum.tile([P, HALF], F32, name=f"{label}{h}")
+        def product(codes, scales, a, b, label):
+            acc = psum.tile([P, b - a], F32, name=label)
             nc.tensor.matmul_mx(out=acc[:], lhsT=codes[:].bitcast(FP8X4), lhsT_scale=scales[:],
-                                rhs=x_w[h][:].bitcast(FP8X4), rhs_scale=x_sc[:, HALF * h : HALF * (h + 1)],
+                                rhs=x_w[:, a:b].bitcast(FP8X4), rhs_scale=x_sc[:, a:b],
                                 start=True, stop=True)
             return acc
 
-        yr_ps = [product(w1_codes, w1_scales, h, "yr") for h in range(2)]
-        yd = [product(w2_codes, w2_scales, h, "yd") for h in range(2)]
+        yr_ps = [product(w1_codes, w1_scales, HALF * h, HALF * (h + 1), f"yr{h}") for h in range(2)]
+        yd = product(w2_codes, w2_scales, 0, S, "yd")
 
         sig = keep.tile([P, S], F32, name="sig")
         lns = keep.tile([P, S], F32, name="lns")
         soft = keep.tile([P, S], F32, name="soft")
-        xsq = keep.tile([P, S], F32, name="xsq")
+        dsq = keep.tile([P, S], F32, name="dsq")
         g0 = keep.tile([P, S], F32, name="g0")
-        yr = keep.tile([P, S], F32, name="yr")
+        yr = keep.tile([P, S], F32, name="yr", tag="w2_bf", align_bytes=64)
+        xw = keep.tile([P, V], F32, name="xw")
+        rd = keep.tile([P, V], F32, name="rd")
+        rd2 = keep.tile([P, V], F32, name="rd2")
         cols = [slice(HALF * h, HALF * (h + 1)) for h in range(2)]
         nc.scalar.copy(yr[:, cols[0]], yr_ps[0][:])
         nc.vector.tensor_copy(yr[:, cols[1]], yr_ps[1][:])
-        for h in range(2):
-            nc.scalar.activation(sig[:, cols[h]], yd[h][:], ACT.Sigmoid, scale=-1.0)
+        nc.scalar.activation(sig[:], yd[:], ACT.Sigmoid, scale=-1.0)
         nc.scalar.activation(lns[:], sig[:], ACT.Ln, bias=TINY)
+        nc.scalar.activation(warm_out[:, 2:3], sig[:, S - 1 : S], ACT.Abs_reciprocal_sqrt, bias=1.0)
 
         me = keep.tile([P, V], F32, name="me")
-        nc.vector.tensor_copy(me[:], yr[:].indirect(who_t[:]))
         me_rep = keep.tile([P, V, D], F32, name="me_rep")
-        nc.vector.tensor_copy(me_rep[:], me[:].unsqueeze(2).to_broadcast([P, V, D]))
+        halves = [slice(V // 2 * h, V // 2 * (h + 1)) for h in range(2)]
+        for h in range(2):
+            nc.vector.tensor_copy(me[:, halves[h]], yr[:].indirect(who_t[:, 8 * h : 8 * (h + 1)]))
+        for h in range(2):
+            nc.vector.tensor_copy(me_rep[:, halves[h], :], me[:, halves[h]].unsqueeze(2).to_broadcast([P, V // 2, D]))
         me_flat = me_rep[:].rearrange("p v d -> p (v d)")
 
-        diff_a = keep.tile([P, 2 * CH], F32, name="diff_a")
-        diff = [diff_a[:, :CH], diff_a[:, CH:], soft[:, :CH], soft[:, CH:]]
+        diff_early = keep.tile([P, 3 * CH], F32, name="diff_early")
+        diff = [diff_early[:, :CH], diff_early[:, CH : 2 * CH], diff_early[:, 2 * CH :], dsq[:, :CH]]
         gw = keep.tile([P, U], F32, name="gw")
         u = keep.tile([P, U], F32, name="u")
         th = keep.tile([P, U], F32, name="th")
         th2 = keep.tile([P, U], F32, name="th2")
         gw2 = keep.tile([P, U], F32, name="gw2")
         gi = keep.tile([P, U], F32, name="gi")
-        games = [slice(CH * c, CH * (c + 1)) for c in range(NCH)]
-        rated = [slice(VCH * c, VCH * (c + 1)) for c in range(NCH)]
+        niv = keep.tile([P, V], F32, name="niv")
+        info = keep.tile([P, V], F32, name="info")
+        amax_early = keep.tile([P, V // 2], F32, name="amax_early")
         lists = [opp_t[:, 16 * c : 16 * (c + 1)] for c in range(NCH)]
 
+        def games(a, b):
+            return slice(CH * a, CH * b)
+
+        def rated(a, b):
+            return slice(VCH * a, VCH * b)
+
         def gather_diff(c):
-            nc.vector.tensor_tensor(diff[c], yr[:].indirect(lists[c]), me_flat[:, games[c]], ALU.subtract)
+            nc.vector.tensor_tensor(diff[c], yr[:].indirect(lists[c]), me_flat[:, games(c, c + 1)], ALU.subtract)
 
         def gather_gw(c):
-            nc.vector.tensor_tensor(gw[:, games[c]], g0[:].indirect(lists[c]), one_t[:, games[c]], ALU.mult)
+            nc.vector.tensor_tensor(gw[:, games(c, c + 1)], g0[:].indirect(lists[c]), one_t[:, games(c, c + 1)], ALU.mult)
 
         def logit(c):
-            nc.vector.tensor_tensor(u[:, games[c]], gw[:, games[c]], diff[c], ALU.mult)
+            nc.vector.tensor_tensor(u[:, games(c, c + 1)], gw[:, games(c, c + 1)], diff[c], ALU.mult)
+
+        def act(dst, src, a, b, func, scale=1.0):
+            nc.scalar.activation(dst[:, games(a, b)], src[:, games(a, b)], func, scale=scale)
+
+        def by_rated(t, a, b):
+            return t[:, games(a, b)].rearrange("p (v d) -> p v d", d=D)
+
+        def game_info(a, b):
+            nc.vector.scalar_tensor_tensor(gi[:, games(a, b)], th2[:, games(a, b)], 1.0, gw2[:, games(a, b)], ALU.subtract, ALU.mult)
+
+        def largest(dst, a, b):
+            nc.vector.tensor_reduce(dst, by_rated(th, a, b), AXIS.X, ALU.max, apply_absolute_value=True)
+
+        def total(a, b):
+            nc.vector.tensor_reduce(niv[:, rated(a, b)], by_rated(gi, a, b), AXIS.X, ALU.add)
 
         gather_diff(0)
         gather_diff(1)
-        for h in range(2):
-            nc.vector.scalar_tensor_tensor(soft[:, cols[h]], lns[:, cols[h]], -1.0, yd[h][:], ALU.mult, ALU.max)
-        for h in range(2):
-            nc.vector.scalar_tensor_tensor(xsq[:, cols[h]], soft[:, cols[h]], 0.6, soft[:, cols[h]], ALU.add, ALU.mult)
-        nc.scalar.activation(g0[:], xsq[:], ACT.Abs_reciprocal_sqrt, scale=0.304, bias=1.0 + 0.304 * 0.09)
-        rd = keep.tile([P, S], F32, name="rd")
-        rd2 = keep.tile([P, S], F32, name="rd2")
-        nc.scalar.activation(rd[:], xsq[:], ACT.Abs_reciprocal_sqrt, bias=0.09)
         gather_diff(2)
+        for h in range(2):
+            nc.vector.scalar_tensor_tensor(soft[:, cols[h]], lns[:, cols[h]], -1.0, yd[:, cols[h]], ALU.mult, ALU.max)
+        for h in range(2):
+            nc.vector.scalar_tensor_tensor(dsq[:, cols[h]], soft[:, cols[h]], 0.6, soft[:, cols[h]], ALU.add, ALU.mult)
+        nc.scalar.activation(g0[:], dsq[:], ACT.Abs_reciprocal_sqrt, scale=0.304, bias=1.0 + 0.304 * 0.09)
+        nc.vector.tensor_copy(xw[:], dsq[:].indirect(who_t[:]))
+        nc.scalar.activation(rd[:], xw[:], ACT.Abs_reciprocal_sqrt, bias=0.09)
+        nc.scalar.activation(warm_out[:, 3:4], xw[:, V - 1 : V], ACT.Tanh)
         gather_gw(0)
         gather_gw(1)
         logit(0)
         logit(1)
-        gather_gw(2)
         gather_diff(3)
-        logit(2)
+        gather_gw(2)
         gather_gw(3)
-
-        amax = keep.tile([P, V], F32, name="amax")
-        niv = keep.tile([P, V], F32, name="niv")
-        info = keep.tile([P, V], F32, name="info")
-
-        def curves(c):
-            nc.scalar.activation(th[:, games[c]], u[:, games[c]], ACT.Tanh, scale=0.5)
-            nc.scalar.activation(gw2[:, games[c]], gw[:, games[c]], ACT.Square)
-            nc.scalar.activation(th2[:, games[c]], th[:, games[c]], ACT.Square)
-
-        def by_rated(t, c):
-            return t[:, games[c]].rearrange("p (v d) -> p v d", d=D)
-
-        def game_info(c):
-            nc.vector.scalar_tensor_tensor(gi[:, games[c]], th2[:, games[c]], 1.0, gw2[:, games[c]], ALU.subtract, ALU.mult)
-
-        def largest(c):
-            nc.vector.tensor_reduce(amax[:, rated[c]], by_rated(th, c), AXIS.X, ALU.max, apply_absolute_value=True)
-
-        def total(c):
-            nc.vector.tensor_reduce(niv[:, rated[c]], by_rated(gi, c), AXIS.X, ALU.add)
+        logit(2)
+        logit(3)
+        act(th, u, 0, 2, ACT.Tanh, 0.5)
+        act(gw2, gw, 0, 2, ACT.Square)
+        act(th2, th, 0, 2, ACT.Square)
+        nc.scalar.activation(rd2[:], rd[:], ACT.Square)
+        act(gw2, gw, 2, 4, ACT.Square)
+        act(th, u, 2, 4, ACT.Tanh, 0.5)
+        act(th2, th, 2, 4, ACT.Square)
+        nc.scalar.activation(warm_out[:, 1:2], th2[:, U - 1 : U], ACT.Abs_reciprocal_sqrt, bias=1.0)
+        root = keep.tile([P, V], F32, name="root")
+        res = keep.tile([P, V], F32, name="res")
 
         def precision(h):
-            half = slice(V // 2 * h, V // 2 * (h + 1))
-            nc.vector.tensor_tensor(info[:, half], rd2[:].indirect(who_t[:, 8 * h : 8 * (h + 1)]), niv[:, half], ALU.subtract)
+            nc.vector.scalar_tensor_tensor(info[:, halves[h]], niv[:, halves[h]], -0.25, rd2[:, halves[h]], ALU.mult, ALU.add)
+            nc.scalar.activation(root[:, halves[h]], info[:, halves[h]], ACT.Abs_reciprocal_sqrt)
 
-        curves(0)
-        game_info(0)
-        logit(3)
-        curves(1)
-        curves(2)
-        nc.scalar.activation(rd2[:], rd[:], ACT.Square, scale=2.0)
-        curves(3)
-        nc.scalar.activation(warm_out[:, 1:2], th2[:, U - 1 : U], ACT.Abs_reciprocal_sqrt, bias=1.0)
-        total(0)
-        game_info(1)
-        largest(0)
-        total(1)
-        game_info(2)
-        largest(1)
-        total(2)
+        def finish(h, amax):
+            nc.vector.scalar_tensor_tensor(res[:, halves[h]], amax, 0.25, root[:, halves[h]], ALU.mult, ALU.add)
+            nc.sync.dma_start(out[:, halves[h]], res[:, halves[h]])
+
+        game_info(0, 2)
+        largest(amax_early[:], 0, 2)
+        total(0, 2)
+        game_info(2, 4)
         precision(0)
-        game_info(3)
-        largest(2)
-        total(3)
-        largest(3)
+        total(2, 4)
         precision(1)
-        root = keep.tile([P, V], F32, name="root")
-        nc.scalar.activation(root[:], info[:], ACT.Abs_reciprocal_sqrt, scale=0.25)
-        res = keep.tile([P, V], F32, name="res")
-        nc.vector.scalar_tensor_tensor(res[:], amax[:], 0.25, root[:], ALU.mult, ALU.add)
-        nc.sync.dma_start(out, res[:])
+        largest(niv[:, halves[1]], 2, 4)
+        finish(0, amax_early[:])
+        finish(1, niv[:, halves[1]])

@@ -43,14 +43,14 @@ def tile_picked_yglick_dev_p_kernel(tc, x_words, x_scales, w1, w2, one, offs, op
         warm = keep.tile([P, 8], F32, name="warm")
         warm_out = keep.tile([P, 8], F32, name="warm_out")
         nc.vector.memset(warm[:], 1.0)
-        nc.scalar.activation(warm_out[:, 0:1], warm[:, 0:1], ACT.Sigmoid)
 
+        nc.scalar.dma_start(w2_raw[:], w2.rearrange("(p j) n -> p j n", j=4))
+        nc.scalar.activation(warm_out[:, 0:1], warm[:, 0:1], ACT.Sigmoid)
         nc.sync.dma_start(offs_t[:], offs)
         nc.sync.dma_start(w1_raw[:], w1.rearrange("(p j) n -> p j n", j=4))
         for q in range(4):
             nc.sync.dma_start(all_scales[32 * q : 32 * q + 4, :].bitcast(I32), x_scales[0, 4 * q : 4 * q + 4, :].bitcast(I32))
         nc.sync.dma_start(all_words[:].bitcast(I32), x_words[0].rearrange("p n t -> p (n t)").bitcast(I32))
-        nc.sync.dma_start(w2_raw[:], w2.rearrange("(p j) n -> p j n", j=4))
         nc.sync.dma_start(who_t[:], who)
         nc.sync.dma_start(opp_t[:], opp)
 
@@ -63,6 +63,7 @@ def tile_picked_yglick_dev_p_kernel(tc, x_words, x_scales, w1, w2, one, offs, op
             return codes, scales
 
         w1_codes, w1_scales = quantise(w1_raw, "w1", nc.vector.tensor_copy)
+        w2_codes, w2_scales = quantise(w2_raw, "w2", nc.vector.tensor_copy)
         one_t = keep.tile([P, U], F32, name="one_t", tag="w1_then_one")
         nc.sync.dma_start(one_t[:], one)
 
@@ -71,7 +72,6 @@ def tile_picked_yglick_dev_p_kernel(tc, x_words, x_scales, w1, w2, one, offs, op
         x_w = keep.tile([P, S], U32, name="x_w", align_bytes=64)
         for h in range(2):
             nc.vector.tensor_copy(x_w[:, HALF * h : HALF * (h + 1)], all_words[:].indirect(offs_t[:, 16 * h : 16 * (h + 1)]))
-        w2_codes, w2_scales = quantise(w2_raw, "w2", nc.scalar.copy)
 
         def product(codes, scales, a, b, label):
             acc = psum.tile([P, b - a], F32, name=label)
@@ -80,22 +80,26 @@ def tile_picked_yglick_dev_p_kernel(tc, x_words, x_scales, w1, w2, one, offs, op
                                 start=True, stop=True)
             return acc
 
-        yr_ps = [product(w1_codes, w1_scales, HALF * h, HALF * (h + 1), f"yr{h}") for h in range(2)]
-        yd = product(w2_codes, w2_scales, 0, S, "yd")
+        yd = []
+        yr_ps = []
+        for h in range(2):
+            yr_ps.append(product(w1_codes, w1_scales, HALF * h, HALF * (h + 1), f"yr{h}"))
+            yd.append(product(w2_codes, w2_scales, HALF * h, HALF * (h + 1), f"yd{h}"))
 
         sig = keep.tile([P, S], F32, name="sig")
         lns = keep.tile([P, S], F32, name="lns")
         soft = keep.tile([P, S], F32, name="soft")
         dsq = keep.tile([P, S], F32, name="dsq")
         g0 = keep.tile([P, S], F32, name="g0")
-        yr = keep.tile([P, S], F32, name="yr", tag="w2_bf", align_bytes=64)
+        yr = keep.tile([P, S], F32, name="yr")
         xw = keep.tile([P, V], F32, name="xw")
         rd = keep.tile([P, V], F32, name="rd")
         rd2 = keep.tile([P, V], F32, name="rd2")
         cols = [slice(HALF * h, HALF * (h + 1)) for h in range(2)]
         nc.scalar.copy(yr[:, cols[0]], yr_ps[0][:])
+        nc.scalar.activation(sig[:, cols[0]], yd[0][:], ACT.Sigmoid, scale=-1.0)
         nc.vector.tensor_copy(yr[:, cols[1]], yr_ps[1][:])
-        nc.scalar.activation(sig[:], yd[:], ACT.Sigmoid, scale=-1.0)
+        nc.scalar.activation(sig[:, cols[1]], yd[1][:], ACT.Sigmoid, scale=-1.0)
         nc.scalar.activation(lns[:], sig[:], ACT.Ln, bias=TINY)
         nc.scalar.activation(warm_out[:, 2:3], sig[:, S - 1 : S], ACT.Abs_reciprocal_sqrt, bias=1.0)
 
@@ -108,8 +112,8 @@ def tile_picked_yglick_dev_p_kernel(tc, x_words, x_scales, w1, w2, one, offs, op
             nc.vector.tensor_copy(me_rep[:, halves[h], :], me[:, halves[h]].unsqueeze(2).to_broadcast([P, V // 2, D]))
         me_flat = me_rep[:].rearrange("p v d -> p (v d)")
 
-        diff_early = keep.tile([P, 3 * CH], F32, name="diff_early")
-        diff = [diff_early[:, :CH], diff_early[:, CH : 2 * CH], diff_early[:, 2 * CH :], dsq[:, :CH]]
+        diff_all = keep.tile([P, U], F32, name="diff_all")
+        diff = [diff_all[:, CH * c : CH * (c + 1)] for c in range(NCH)]
         gw = keep.tile([P, U], F32, name="gw")
         u = keep.tile([P, U], F32, name="u")
         th = keep.tile([P, U], F32, name="th")
@@ -154,8 +158,9 @@ def tile_picked_yglick_dev_p_kernel(tc, x_words, x_scales, w1, w2, one, offs, op
         gather_diff(0)
         gather_diff(1)
         gather_diff(2)
+        gather_diff(3)
         for h in range(2):
-            nc.vector.scalar_tensor_tensor(soft[:, cols[h]], lns[:, cols[h]], -1.0, yd[:, cols[h]], ALU.mult, ALU.max)
+            nc.vector.scalar_tensor_tensor(soft[:, cols[h]], lns[:, cols[h]], -1.0, yd[h][:], ALU.mult, ALU.max)
         for h in range(2):
             nc.vector.scalar_tensor_tensor(dsq[:, cols[h]], soft[:, cols[h]], 0.6, soft[:, cols[h]], ALU.add, ALU.mult)
         nc.scalar.activation(g0[:], dsq[:], ACT.Abs_reciprocal_sqrt, scale=0.304, bias=1.0 + 0.304 * 0.09)
@@ -166,7 +171,6 @@ def tile_picked_yglick_dev_p_kernel(tc, x_words, x_scales, w1, w2, one, offs, op
         gather_gw(1)
         logit(0)
         logit(1)
-        gather_diff(3)
         gather_gw(2)
         gather_gw(3)
         logit(2)
@@ -175,9 +179,11 @@ def tile_picked_yglick_dev_p_kernel(tc, x_words, x_scales, w1, w2, one, offs, op
         act(gw2, gw, 0, 2, ACT.Square)
         act(th2, th, 0, 2, ACT.Square)
         nc.scalar.activation(rd2[:], rd[:], ACT.Square)
-        act(gw2, gw, 2, 4, ACT.Square)
-        act(th, u, 2, 4, ACT.Tanh, 0.5)
-        act(th2, th, 2, 4, ACT.Square)
+        act(gw2, gw, 2, 3, ACT.Square)
+        act(th, u, 2, 3, ACT.Tanh, 0.5)
+        act(th, u, 3, 4, ACT.Tanh, 0.5)
+        act(th2, th, 2, 3, ACT.Square)
+        act(th2, th, 3, 4, ACT.Square)
         nc.scalar.activation(warm_out[:, 1:2], th2[:, U - 1 : U], ACT.Abs_reciprocal_sqrt, bias=1.0)
         root = keep.tile([P, V], F32, name="root")
         res = keep.tile([P, V], F32, name="res")
@@ -190,10 +196,12 @@ def tile_picked_yglick_dev_p_kernel(tc, x_words, x_scales, w1, w2, one, offs, op
             nc.vector.scalar_tensor_tensor(res[:, halves[h]], amax, 0.25, root[:, halves[h]], ALU.mult, ALU.add)
             nc.sync.dma_start(out[:, halves[h]], res[:, halves[h]])
 
-        game_info(0, 2)
+        nc.vector.tensor_tensor(gw2[:, games(3, 4)], gw[:, games(3, 4)], gw[:, games(3, 4)], ALU.mult)
         largest(amax_early[:], 0, 2)
+        game_info(0, 2)
+        game_info(2, 3)
         total(0, 2)
-        game_info(2, 4)
+        game_info(3, 4)
         precision(0)
         total(2, 4)
         precision(1)

from contextlib import ExitStack

import concourse.mybir as mybir

K, T, S, N, D, V, U = 512, 2048, 512, 128, 4, 256, 1024
P = 128
FLOPS = 2 * 2 * K * N * S

F32 = mybir.dt.float32
BF16 = mybir.dt.bfloat16
I32 = mybir.dt.int32
U32 = mybir.dt.uint32
U16 = mybir.dt.uint16
U8 = mybir.dt.uint8
FP8X4 = mybir.dt.float8_e4m3fn_x4
ALU = mybir.AluOpType
ACT = mybir.ActivationFunctionType
AXIS = mybir.AxisListType

HALF = S // 2
CH = 256
NCH = U // CH
VCH = CH // D
TINY = 2.0 ** -60


def tile_picked_yglick_dev_p_kernel(tc, x_words, x_scales, w1, w2, one, offs, opp, who, out):
    nc = tc.nc
    with ExitStack() as ctx:
        keep = ctx.enter_context(tc.tile_pool(name="keep", bufs=1))
        psum = ctx.enter_context(tc.psum_pool(name="psum", bufs=1))

        offs_t = keep.tile([P, S // 16], U16, name="offs_t")
        opp_t = keep.tile([P, U // 16], U16, name="opp_t")
        who_t = keep.tile([P, V // 16], U16, name="who_t")
        all_scales = keep.tile([P, T], U8, name="all_scales", align_bytes=64)
        all_words = keep.tile([P, T], U32, name="all_words", align_bytes=64)
        w1_raw = keep.tile([P, 4, N], F32, name="w1_raw", tag="w1_then_one")
        w2_raw = keep.tile([P, 4, N], F32, name="w2_raw")

        nc.vector.memset(all_scales[:, : T // 2].bitcast(I32), 0)
        nc.gpsimd.memset(all_scales[:, T // 2 :].bitcast(I32), 0)
        warm = keep.tile([P, 8], F32, name="warm")
        warm_out = keep.tile([P, 8], F32, name="warm_out")
        nc.vector.memset(warm[:], 1.0)

        nc.scalar.dma_start(w2_raw[:], w2.rearrange("(p j) n -> p j n", j=4))
        nc.scalar.activation(warm_out[:, 0:1], warm[:, 0:1], ACT.Sigmoid)
        nc.sync.dma_start(offs_t[:], offs)
        nc.sync.dma_start(w1_raw[:], w1.rearrange("(p j) n -> p j n", j=4))
        for q in range(4):
            nc.sync.dma_start(all_scales[32 * q : 32 * q + 4, :].bitcast(I32), x_scales[0, 4 * q : 4 * q + 4, :].bitcast(I32))
        nc.sync.dma_start(all_words[:].bitcast(I32), x_words[0].rearrange("p n t -> p (n t)").bitcast(I32))
        nc.sync.dma_start(who_t[:], who)
        nc.sync.dma_start(opp_t[:], opp)

        def quantise(raw, label, copy):
            grouped = keep.tile([P, N, 4], BF16, name=label + "_bf", tag=label + "_bf", align_bytes=64)
            copy(grouped[:].rearrange("p (c i) j -> p c j i", i=4), raw[:].rearrange("p j (c i) -> p c j i", i=4))
            codes = keep.tile([P, N], U32, name=label + "_codes", align_bytes=64)
            scales = keep.tile([P, N], U8, name=label + "_scales", align_bytes=64)
            nc.vector.quantize_mx(out=codes[:].bitcast(FP8X4), scales=scales[:], in_=grouped[:].rearrange("p n j -> p (n j)"))
            return codes, scales

        w1_codes, w1_scales = quantise(w1_raw, "w1", nc.vector.tensor_copy)
        w2_codes, w2_scales = quantise(w2_raw, "w2", nc.vector.tensor_copy)
        one_t = keep.tile([P, U], F32, name="one_t", tag="w1_then_one")
        nc.sync.dma_start(one_t[:], one)

        x_sc = keep.tile([P, S], U8, name="x_sc", align_bytes=64)
        nc.vector.tensor_copy(x_sc[:], all_scales[:].indirect(offs_t[:]))
        x_w = keep.tile([P, S], U32, name="x_w", align_bytes=64)
        for h in range(2):
            nc.vector.tensor_copy(x_w[:, HALF * h : HALF * (h + 1)], all_words[:].indirect(offs_t[:, 16 * h : 16 * (h + 1)]))

        def product(codes, scales, a, b, label):
            acc = psum.tile([P, b - a], F32, name=label)
            nc.tensor.matmul_mx(out=acc[:], lhsT=codes[:].bitcast(FP8X4), lhsT_scale=scales[:],
                                rhs=x_w[:, a:b].bitcast(FP8X4), rhs_scale=x_sc[:, a:b],
                                start=True, stop=True)
            return acc

        yd = []
        yr_ps = []
        for h in range(2):
            yr_ps.append(product(w1_codes, w1_scales, HALF * h, HALF * (h + 1), f"yr{h}"))
            yd.append(product(w2_codes, w2_scales, HALF * h, HALF * (h + 1), f"yd{h}"))

        sig = keep.tile([P, S], F32, name="sig")
        lns = keep.tile([P, S], F32, name="lns")
        soft = keep.tile([P, S], F32, name="soft")
        dsq = keep.tile([P, S], F32, name="dsq")
        g0 = keep.tile([P, S], F32, name="g0")
        yr = keep.tile([P, S], F32, name="yr")
        xw = keep.tile([P, V], F32, name="xw")
        rd = keep.tile([P, V], F32, name="rd")
        rd2 = keep.tile([P, V], F32, name="rd2")
        cols = [slice(HALF * h, HALF * (h + 1)) for h in range(2)]
        nc.scalar.copy(yr[:, cols[0]], yr_ps[0][:])
        nc.scalar.activation(sig[:, cols[0]], yd[0][:], ACT.Sigmoid, scale=-1.0)
        nc.vector.tensor_copy(yr[:, cols[1]], yr_ps[1][:])
        nc.scalar.activation(sig[:, cols[1]], yd[1][:], ACT.Sigmoid, scale=-1.0)
        nc.scalar.activation(lns[:], sig[:], ACT.Ln, bias=TINY)
        nc.scalar.activation(warm_out[:, 2:3], sig[:, S - 1 : S], ACT.Abs_reciprocal_sqrt, bias=1.0)

        me = keep.tile([P, V], F32, name="me")
        me_rep = keep.tile([P, V, D], F32, name="me_rep")
        halves = [slice(V // 2 * h, V // 2 * (h + 1)) for h in range(2)]
        for h in range(2):
            nc.vector.tensor_copy(me[:, halves[h]], yr[:].indirect(who_t[:, 8 * h : 8 * (h + 1)]))
        for h in range(2):
            nc.vector.tensor_copy(me_rep[:, halves[h], :], me[:, halves[h]].unsqueeze(2).to_broadcast([P, V // 2, D]))
        me_flat = me_rep[:].rearrange("p v d -> p (v d)")

        diff_all = keep.tile([P, U], F32, name="diff_all")
        diff = [diff_all[:, CH * c : CH * (c + 1)] for c in range(NCH)]
        gw = keep.tile([P, U], F32, name="gw")
        u = keep.tile([P, U], F32, name="u")
        th = keep.tile([P, U], F32, name="th")
        th2 = keep.tile([P, U], F32, name="th2")
        gw2 = keep.tile([P, U], F32, name="gw2")
        gi = keep.tile([P, U], F32, name="gi")
        niv = keep.tile([P, V], F32, name="niv")
        info = keep.tile([P, V], F32, name="info")
        amax_early = keep.tile([P, V // 2], F32, name="amax_early")
        lists = [opp_t[:, 16 * c : 16 * (c + 1)] for c in range(NCH)]

        def games(a, b):
            return slice(CH * a, CH * b)

        def rated(a, b):
            return slice(VCH * a, VCH * b)

        def gather_diff(c):
            nc.vector.tensor_tensor(diff[c], yr[:].indirect(lists[c]), me_flat[:, games(c, c + 1)], ALU.subtract)

        def gather_gw(c):
            nc.vector.tensor_tensor(gw[:, games(c, c + 1)], g0[:].indirect(lists[c]), one_t[:, games(c, c + 1)], ALU.mult)

        def logit(c):
            nc.vector.tensor_tensor(u[:, games(c, c + 1)], gw[:, games(c, c + 1)], diff[c], ALU.mult)

        def act(dst, src, a, b, func, scale=1.0):
            nc.scalar.activation(dst[:, games(a, b)], src[:, games(a, b)], func, scale=scale)

        def by_rated(t, a, b):
            return t[:, games(a, b)].rearrange("p (v d) -> p v d", d=D)

        def game_info(a, b):
            nc.vector.scalar_tensor_tensor(gi[:, games(a, b)], th2[:, games(a, b)], 1.0, gw2[:, games(a, b)], ALU.subtract, ALU.mult)

        def largest(dst, a, b):
            nc.vector.tensor_reduce(dst, by_rated(th, a, b), AXIS.X, ALU.max, apply_absolute_value=True)

        def total(a, b):
            nc.vector.tensor_reduce(niv[:, rated(a, b)], by_rated(gi, a, b), AXIS.X, ALU.add)

        gather_diff(0)
        gather_diff(1)
        gather_diff(2)
        gather_diff(3)
        for h in range(2):
            nc.vector.scalar_tensor_tensor(soft[:, cols[h]], lns[:, cols[h]], -1.0, yd[h][:], ALU.mult, ALU.max)
        for h in range(2):
            nc.vector.scalar_tensor_tensor(dsq[:, cols[h]], soft[:, cols[h]], 0.6, soft[:, cols[h]], ALU.add, ALU.mult)
        nc.scalar.activation(g0[:], dsq[:], ACT.Abs_reciprocal_sqrt, scale=0.304, bias=1.0 + 0.304 * 0.09)
        nc.vector.tensor_copy(xw[:], dsq[:].indirect(who_t[:]))
        nc.scalar.activation(rd[:], xw[:], ACT.Abs_reciprocal_sqrt, bias=0.09)
        nc.scalar.activation(warm_out[:, 3:4], xw[:, V - 1 : V], ACT.Tanh)
        gather_gw(0)
        gather_gw(1)
        logit(0)
        logit(1)
        gather_gw(2)
        gather_gw(3)
        logit(2)
        logit(3)
        act(th, u, 0, 2, ACT.Tanh, 0.5)
        act(gw2, gw, 0, 2, ACT.Square)
        act(th2, th, 0, 2, ACT.Square)
        nc.scalar.activation(rd2[:], rd[:], ACT.Square)
        act(gw2, gw, 2, 3, ACT.Square)
        act(th, u, 2, 3, ACT.Tanh, 0.5)
        act(th, u, 3, 4, ACT.Tanh, 0.5)
        act(th2, th, 2, 3, ACT.Square)
        act(th2, th, 3, 4, ACT.Square)
        nc.scalar.activation(warm_out[:, 1:2], th2[:, U - 1 : U], ACT.Abs_reciprocal_sqrt, bias=1.0)
        root = keep.tile([P, V], F32, name="root")
        res = keep.tile([P, V], F32, name="res")

        def precision(h):
            nc.vector.scalar_tensor_tensor(info[:, halves[h]], niv[:, halves[h]], -0.25, rd2[:, halves[h]], ALU.mult, ALU.add)
            nc.scalar.activation(root[:, halves[h]], info[:, halves[h]], ACT.Abs_reciprocal_sqrt)

        def finish(h, amax):
            nc.vector.scalar_tensor_tensor(res[:, halves[h]], amax, 0.25, root[:, halves[h]], ALU.mult, ALU.add)
            nc.sync.dma_start(out[:, halves[h]], res[:, halves[h]])

        nc.vector.tensor_tensor(gw2[:, games(3, 4)], gw[:, games(3, 4)], gw[:, games(3, 4)], ALU.mult)
        largest(amax_early[:], 0, 2)
        game_info(0, 2)
        game_info(2, 3)
        total(0, 2)
        game_info(3, 4)
        precision(0)
        total(2, 4)
        precision(1)
        largest(niv[:, halves[1]], 2, 4)
        finish(0, amax_early[:])
        finish(1, niv[:, halves[1]])
